import numpy as np
import ml_dtypes


def mxq(x, axis, fmt="e4m3"):
    dtype, down = {"e4m3": (ml_dtypes.float8_e4m3fn, 7), "e5m2": (ml_dtypes.float8_e5m2, 14)}[fmt]
    v = np.moveaxis(np.asarray(x, np.float32).astype(ml_dtypes.bfloat16).astype(np.float64), axis, -1)
    blocks = v.reshape(v.shape[:-1] + (-1, 32))
    amax = np.abs(blocks).max(-1, keepdims=True)
    byte = np.maximum(np.where(amax > 0, np.frexp(amax)[1] - 1 + 127, 0) - down, 1)
    scale = np.exp2(byte - 127.0)
    codes = (blocks / scale).astype(np.float32).astype(dtype).astype(np.float64)
    return np.moveaxis((codes * scale).reshape(v.shape), -1, axis)


WIDE = False


def mx_kscale(k):
    if not WIDE:
        return np.ones(k)
    levels = np.array([10, -10, 5, -5, 0])
    if k % 512:
        return np.exp2(np.random.permutation(np.resize(levels, k // 32))).repeat(32)
    a = np.empty((k // 512, 16))
    for p in range(k // 512):
        a[p, :8] = np.random.permutation(np.resize(levels, 8))
        for g in range(8):
            far = levels[np.abs(levels - a[p, g]) >= 10]
            a[p, g + 8] = far[np.random.randint(len(far))]
    return np.exp2(a.ravel()).repeat(32)


def f64(x):
    return np.asarray(x).astype(np.float64)


def striped(idx):
    return np.tile(idx.reshape(-1, 16).T, (8, 1)).astype(np.uint16)


def unstriped(offs):
    return offs[:16].T.reshape(-1).astype(np.int64)


def striped8(idx):
    return np.concatenate([x.reshape(-1, 16).T for x in idx]).astype(np.uint16)


def runs(offs, k):
    lists = np.stack([offs[16 * r : 16 * r + 16].T.reshape(-1) for r in range(8)]).astype(np.int64)
    return lists[np.arange(k) % 512 // 64]


def pack_weight(w):
    k, n = w.shape
    w = f64(np.asarray(w, np.float32).astype(ml_dtypes.bfloat16)).reshape(k // 32, 32, n)
    amax = np.abs(w).max(1)
    byte = np.clip(np.where(amax > 0, np.frexp(amax)[1] - 1 + 127 - 7, 1), 1, 254)
    scaled = (w * np.exp2(127.0 - byte)[:, None, :]).reshape(k, n).astype(np.float32)
    words = np.ascontiguousarray(scaled.reshape(k // 512, 128, 4, n).transpose(0, 1, 3, 2)).astype(ml_dtypes.float8_e4m3fn).view(np.uint8)
    return words, np.ascontiguousarray(byte.astype(np.uint8).reshape(k // 512, 16, n))


def unpack_weight(words, scales):
    g, p, n, _ = words.shape
    vals = np.ascontiguousarray(words).view(ml_dtypes.float8_e4m3fn).astype(np.float64) * np.repeat(np.exp2(scales.astype(np.float64) - 127.0), 8, axis=1)[..., None]
    return vals.transpose(0, 1, 3, 2).reshape(g * 512, n)


K, T, S, H, C = 512, 2048, 512, 512, 512


def setup_inputs():
    n = np.random.standard_normal
    s = mx_kscale(K)[:, None]
    packed_xT = pack_weight(n((K, T)) * s)
    return {
        "x_words": packed_xT[0],
        "x_scales": packed_xT[1],
        "w1": (n((K, H)) / np.sqrt(K) / s).astype(np.float32),
        "w2": (n((K, H)) / np.sqrt(K) / s).astype(np.float32),
        "w3": (n((K, H)) / np.sqrt(K) / s).astype(np.float32),
        "gs": (np.random.uniform(0.5, 1.5, (K, 1)) / s).astype(np.float32),
        "offs": striped(np.random.permutation(T)[:S]),
        "two": striped(np.random.permutation(T)[:S]),
        "thr": striped(np.random.permutation(T)[:S]),
        "di": striped8(np.stack([np.random.permutation(S) for _ in range(8)])),
        "dj": striped8(np.stack([np.random.permutation(S) for _ in range(8)])),
        "dk": striped8(np.stack([np.random.permutation(S) for _ in range(8)])),
        "col": striped8(np.random.randint(0, S, (8, S))),
        "cand": striped(np.random.permutation(T)[:C]),
    }


def reference(x_words, x_scales, w1, w2, w3, gs, offs, two, thr, di, dj, dk, col, cand):
    x_cand = unpack_weight(x_words, x_scales)[:, unstriped(cand)]
    xq = unpack_weight(x_words, x_scales)[:, unstriped(offs)]
    y = mxq(f64(w1), 0, "e4m3").T @ xq
    x_two = unpack_weight(x_words, x_scales)[:, unstriped(two)]
    c = mxq(f64(w2), 0, "e4m3").T @ x_two
    x_thr = unpack_weight(x_words, x_scales)[:, unstriped(thr)]
    rf = mxq(f64(w3), 0, "e4m3").T @ x_thr
    z = f64(gs) * (np.minimum(np.minimum(y[np.arange(H)[:, None], runs(di, H)], y[np.arange(H)[:, None], runs(dj, H)]), y[np.arange(H)[:, None], runs(dk, H)]) + np.abs(c - (rf[np.arange(H)[:, None], runs(col, H)])))
    return 0.0625 * ((x_cand.T @ mxq(z, 0, "e4m3")))

@@ -1,0 +1,230 @@
+from contextlib import ExitStack
+
+import concourse.mybir as mybir
+from concourse.masks import make_identity
+
+K, T, S, H, C = 512, 2048, 512, 512, 512
+FLOPS = 2 * K * (3 * H * S + C * S)
+
+F32 = mybir.dt.float32
+BF16 = mybir.dt.bfloat16
+I32 = mybir.dt.int32
+U32 = mybir.dt.uint32
+U16 = mybir.dt.uint16
+U8 = mybir.dt.uint8
+FP8X4 = mybir.dt.float8_e4m3fn_x4
+ALU = mybir.AluOpType
+ACT = mybir.ActivationFunctionType
+
+P = 128
+PACK = 4
+STRIPE = 16
+HEAD = 384
+OUT_SCALE = 0.0625
+
+
+def tile_picked_dtwcell_none_p_kernel(tc, x_words, x_scales, w1, w2, w3, gs, offs, two, thr, di, dj, dk, col, cand, out):
+    nc = tc.nc
+    with ExitStack() as ctx:
+        keep = ctx.enter_context(tc.tile_pool(name="keep", bufs=1))
+        ring = ctx.enter_context(tc.tile_pool(name="ring", bufs=2))
+        psum = ctx.enter_context(tc.psum_pool(name="psum", bufs=1))
+
+        def load_list(name, src):
+            tile = keep.tile([P, S // STRIPE], U16, name="list_" + name)
+            nc.sync.dma_start(tile[:], src)
+            return tile
+
+        def load_weight(name, src):
+            raw = keep.tile([P, PACK, H], F32, name="raw_" + name)
+            nc.sync.dma_start(raw[:], src.rearrange("(p j) c -> p j c", j=PACK))
+            return raw
+
+        table_scales = keep.tile([P, T], U8, name="table_scales", align_bytes=64)
+        nc.vector.memset(table_scales[:].bitcast(I32), 0)
+        for q in range(4):
+            nc.sync.dma_start(
+                table_scales[32 * q : 32 * q + 4, :].bitcast(I32),
+                x_scales[0, 4 * q : 4 * q + 4, :].bitcast(I32),
+            )
+        lists = {}
+        for name, src in (("thr", thr), ("offs", offs), ("two", two)):
+            lists[name] = load_list(name, src)
+        raw = {"w3": load_weight("w3", w3)}
+        table_words = keep.tile([P, T], I32, name="table_words", align_bytes=64)
+        nc.sync.dma_start(table_words[:], x_words[0].rearrange("p n r -> p (n r)").bitcast(I32))
+        lists["cand"] = load_list("cand", cand)
+        raw["w1"] = load_weight("w1", w1)
+        for name, src in (("col", col), ("di", di), ("dj", dj), ("dk", dk)):
+            lists[name] = load_list(name, src)
+        gain = keep.tile([P, PACK], F32, name="gain")
+        nc.sync.dma_start(gain[:], gs.rearrange("(p t) o -> p (t o)", t=PACK))
+        raw["w2"] = load_weight("w2", w2)
+
+        ident = keep.tile([P, P], F32, name="ident")
+        make_identity(nc, ident[:])
+
+        picked_scales, picked_words = {}, {}
+
+        def pick_scales(name):
+            tile = keep.tile([P, S], U8, name="scales_" + name, align_bytes=64)
+            nc.vector.tensor_copy(tile[:], table_scales[:].indirect(lists[name][:]))
+            picked_scales[name] = tile
+
+        def pick_words(name, slot):
+            tile = keep.tile([P, S], U32, name="words_" + name, tag=slot, align_bytes=64)
+            nc.vector.tensor_copy(tile[:], table_words[:].bitcast(U32).indirect(lists[name][:]))
+            picked_words[name] = tile
+
+        def quantise_weight(name):
+            dealt = keep.tile([P, PACK, P, PACK], BF16, name="dealt_" + name, tag="dealt_" + name, align_bytes=64)
+            nc.scalar.copy(
+                dealt[:].rearrange("p t m j -> p m j t"),
+                raw[name][:].rearrange("p j (m t) -> p m j t", t=PACK),
+            )
+            codes = keep.tile([P, H], U32, name="codes_" + name, align_bytes=64)
+            scales = keep.tile([P, H], U8, name="wscales_" + name, align_bytes=64)
+            nc.vector.quantize_mx(codes[:].bitcast(FP8X4), scales[:], dealt[:].rearrange("p t m j -> p (t m j)"))
+            return codes, scales
+
+        def project(weight, name, first_bank, result, sign):
+            codes, scales = weight
+            tiles = []
+            for t in range(PACK):
+                bank = psum.tile([P, S], F32, name="bank%d" % (first_bank + t))
+                cols = slice(t * P, (t + 1) * P)
+                nc.tensor.matmul_mx(
+                    out=bank[:],
+                    lhsT=codes[:, cols].bitcast(FP8X4),
+                    lhsT_scale=scales[:, cols],
+                    rhs=picked_words[name][:].bitcast(FP8X4),
+                    rhs_scale=picked_scales[name][:],
+                    start=True,
+                    stop=True,
+                )
+                tile = keep.tile([P, S], F32, name="%s%d" % (result, t))
+                nc.scalar.activation(tile[:], bank[:], ACT.Copy, scale=sign)
+                tiles.append(tile)
+            return tiles
+
+        def gather(dst, window, name, lo, hi):
+            nc.vector.tensor_copy(dst, window[:].indirect(lists[name][:, lo // STRIPE : hi // STRIPE]))
+
+        for name in ("thr", "offs", "two", "cand"):
+            pick_scales(name)
+        w3q = quantise_weight("w3")
+        pick_words("thr", "words_thr")
+        ref = project(w3q, "thr", 0, "ref", 1.0)
+        pick_words("offs", "dealt_w3")
+        pick_words("two", "words_two")
+        pick_words("cand", "words_cand")
+        w1q = quantise_weight("w1")
+        cost = project(w1q, "offs", 4, "cost", 1.0)
+        fetched = []
+        for t in range(PACK):
+            tile = keep.tile([P, S], F32, name="fetched%d" % t, tag="dealt_w1" if t == 1 else "fetched%d" % t, align_bytes=64)
+            for lo in range(0, S, S // 2):
+                gather(tile[:, lo : lo + S // 2], ref[t], "col", lo, lo + S // 2)
+            fetched.append(tile)
+        w2q = quantise_weight("w2")
+        minus_frame = project(w2q, "two", 0, "minus_frame", -1.0)
+
+        dist = []
+        for t in range(PACK):
+            diff = psum.tile([P, S // P, P], F32, name="bank%d" % (4 + t))
+            for b in range(S // P):
+                cols = slice(b * P, (b + 1) * P)
+                nc.tensor.matmul(diff[:, b, :], fetched[t][:, cols], ident[:], start=True, stop=False, is_transpose=True)
+                nc.tensor.matmul(diff[:, b, :], minus_frame[t][:, cols], ident[:], start=False, stop=True, is_transpose=True)
+            size = ring.tile([P, S // P, P], F32, name="size")
+            nc.scalar.activation(size[:], diff[:], ACT.Abs)
+            back = psum.tile([P, S], F32, name="bank%d" % t)
+            for b in range(S // P):
+                nc.tensor.transpose(back[:, b * P : (b + 1) * P], size[:, b, :], ident[:])
+            weighted = keep.tile([P, S], F32, name="dist%d" % t)
+            nc.scalar.activation(weighted[:], back[:], ACT.Copy, scale=gain[:, t : t + 1])
+            dist.append(weighted)
+
+        z_head = keep.tile([P, PACK, HEAD], F32, name="z_head")
+        z_tail = keep.tile([P, PACK, S - HEAD], F32, name="z_tail")
+        steps = [(z_head, 0, HEAD, t) for t in range(PACK)] + [(z_tail, HEAD, S, t) for t in range(PACK)]
+        state = {}
+
+        def cell(n, name):
+            z4, lo, hi, t = steps[n]
+            if (n, name) == (6, "dk"):
+                tile = keep.tile([P, hi - lo], F32, name="cell6", tag="woven0", align_bytes=64)
+            elif (n, name) == (7, "dj"):
+                tile = keep.tile([P, hi - lo], F32, name="cell7", tag="woven256", align_bytes=64)
+            else:
+                tile = ring.tile([P, hi - lo], F32, name="cell_" + name)
+            gather(tile[:], cost[t], name, lo, hi)
+            state[n, name] = tile
+
+        def least_of(n, first, second, result):
+            z4, lo, hi, t = steps[n]
+            tile = ring.tile([P, hi - lo], F32, name=result)
+            nc.vector.tensor_tensor(tile[:], state[n, first][:], state[n, second][:], ALU.min)
+            state[n, result] = tile
+
+        def weigh(n):
+            z4, lo, hi, t = steps[n]
+            nc.vector.scalar_tensor_tensor(
+                z4[:, t, :], state[n, "least"][:], gain[:, t : t + 1], dist[t][:, lo:hi], ALU.mult, ALU.add
+            )
+
+        def quantise_z(z4, a, b, base, weave):
+            woven = keep.tile([P, b - a, PACK], BF16, name="woven%d" % (base + a), tag="woven%d" % (base + a), align_bytes=64)
+            weave(woven[:], z4[:, :, a:b].rearrange("p t j -> p j t"))
+            codes = keep.tile([P, b - a], U32, name="zcodes%d" % (base + a), align_bytes=64)
+            scales = keep.tile([P, b - a], U8, name="zscales%d" % (base + a), align_bytes=64)
+            nc.vector.quantize_mx(codes[:].bitcast(FP8X4), scales[:], woven[:].rearrange("p j t -> p (j t)"))
+            return codes, scales
+
+        def score(acc, blk, zq):
+            rows = slice(blk * P, (blk + 1) * P)
+            nc.tensor.matmul_mx(
+                out=acc,
+                lhsT=picked_words["cand"][:, rows].bitcast(FP8X4),
+                lhsT_scale=picked_scales["cand"][:, rows],
+                rhs=zq[0][:].bitcast(FP8X4),
+                rhs_scale=zq[1][:],
+                start=True,
+                stop=True,
+            )
+
+        def finish_head():
+            pieces = ((0, 256), (256, HEAD))
+            zq = [quantise_z(z_head, a, b, 0, nc.scalar.copy) for a, b in pieces]
+            result = keep.tile([P, C // P, HEAD], F32, name="result_head")
+            for blk in range(C // P):
+                acc = psum.tile([P, S], F32, name="bank%d" % (4 + blk))
+                for (a, b), piece in zip(pieces, zq):
+                    score(acc[:, a:b], blk, piece)
+                nc.scalar.activation(result[:, blk, :], acc[:, :HEAD], ACT.Copy, scale=OUT_SCALE)
+            nc.sync.dma_start(out[:, :HEAD].rearrange("(b p) j -> p b j", p=P), result[:])
+
+        def finish_tail():
+            zq = quantise_z(z_tail, 0, S - HEAD, HEAD, nc.vector.tensor_copy)
+            result = keep.tile([P, C // P, S - HEAD], F32, name="result_tail")
+            acc = psum.tile([P, C // P, S - HEAD], F32, name="bank0")
+            for blk in range(C // P):
+                score(acc[:, blk, :], blk, zq)
+            nc.scalar.activation(result[:], acc[:], ACT.Copy, scale=OUT_SCALE)
+            nc.sync.dma_start(out[:, HEAD:].rearrange("(b p) j -> p b j", p=P), result[:])
+
+        for n in range(len(steps)):
+            cell(n, "di")
+            cell(n, "dj")
+            if n > 0:
+                least_of(n - 1, "pair", "dk", "least")
+            cell(n, "dk")
+            least_of(n, "di", "dj", "pair")
+            if n > 0:
+                weigh(n - 1)
+            if n == PACK:
+                finish_head()
+        last = len(steps) - 1
+        least_of(last, "pair", "dk", "least")
+        weigh(last)
+        finish_tail()

@@ -20,6 +20,7 @@ P = 128
 PACK = 4
 STRIPE = 16
 HEAD = 384
+ON_TENSOR = 3
 OUT_SCALE = 0.0625
 
 
@@ -48,12 +49,13 @@ def tile_picked_dtwcell_none_p_kernel(tc, x_words, x_scales, w1, w2, w3, gs, off
                 x_scales[0, 4 * q : 4 * q + 4, :].bitcast(I32),
             )
         lists = {}
-        for name, src in (("thr", thr), ("offs", offs), ("two", two)):
+        for name, src in (("thr", thr), ("offs", offs)):
             lists[name] = load_list(name, src)
-        raw = {"w3": load_weight("w3", w3)}
         table_words = keep.tile([P, T], I32, name="table_words", align_bytes=64)
         nc.sync.dma_start(table_words[:], x_words[0].rearrange("p n r -> p (n r)").bitcast(I32))
-        lists["cand"] = load_list("cand", cand)
+        raw = {"w3": load_weight("w3", w3)}
+        for name, src in (("two", two), ("cand", cand)):
+            lists[name] = load_list(name, src)
         raw["w1"] = load_weight("w1", w1)
         for name, src in (("col", col), ("di", di), ("dj", dj), ("dk", dk)):
             lists[name] = load_list(name, src)
@@ -76,12 +78,15 @@ def tile_picked_dtwcell_none_p_kernel(tc, x_words, x_scales, w1, w2, w3, gs, off
             nc.vector.tensor_copy(tile[:], table_words[:].bitcast(U32).indirect(lists[name][:]))
             picked_words[name] = tile
 
-        def quantise_weight(name):
+        def deal_weight(name):
             dealt = keep.tile([P, PACK, P, PACK], BF16, name="dealt_" + name, tag="dealt_" + name, align_bytes=64)
             nc.scalar.copy(
                 dealt[:].rearrange("p t m j -> p m j t"),
                 raw[name][:].rearrange("p j (m t) -> p m j t", t=PACK),
             )
+            return dealt
+
+        def quantise_weight(name, dealt):
             codes = keep.tile([P, H], U32, name="codes_" + name, align_bytes=64)
             scales = keep.tile([P, H], U8, name="wscales_" + name, align_bytes=64)
             nc.vector.quantize_mx(codes[:].bitcast(FP8X4), scales[:], dealt[:].rearrange("p t m j -> p (t m j)"))
@@ -110,15 +115,18 @@ def tile_picked_dtwcell_none_p_kernel(tc, x_words, x_scales, w1, w2, w3, gs, off
         def gather(dst, window, name, lo, hi):
             nc.vector.tensor_copy(dst, window[:].indirect(lists[name][:, lo // STRIPE : hi // STRIPE]))
 
-        for name in ("thr", "offs", "two", "cand"):
+        for name in ("thr", "offs"):
             pick_scales(name)
-        w3q = quantise_weight("w3")
-        pick_words("thr", "words_thr")
-        ref = project(w3q, "thr", 0, "ref", 1.0)
-        pick_words("offs", "dealt_w3")
-        pick_words("two", "words_two")
+        for name in ("thr", "offs"):
+            pick_words(name, "words_" + name)
+        for name in ("two", "cand"):
+            pick_scales(name)
         pick_words("cand", "words_cand")
-        w1q = quantise_weight("w1")
+        w3q = quantise_weight("w3", deal_weight("w3"))
+        ref = project(w3q, "thr", 0, "ref", 1.0)
+        pick_words("two", "dealt_w3")
+        w1q = quantise_weight("w1", deal_weight("w1"))
+        dealt_w2 = deal_weight("w2")
         cost = project(w1q, "offs", 4, "cost", 1.0)
         fetched = []
         for t in range(PACK):
@@ -126,24 +134,26 @@ def tile_picked_dtwcell_none_p_kernel(tc, x_words, x_scales, w1, w2, w3, gs, off
             for lo in range(0, S, S // 2):
                 gather(tile[:, lo : lo + S // 2], ref[t], "col", lo, lo + S // 2)
             fetched.append(tile)
-        w2q = quantise_weight("w2")
+        w2q = quantise_weight("w2", dealt_w2)
         minus_frame = project(w2q, "two", 0, "minus_frame", -1.0)
 
-        dist = []
+        sizes, dist = [], {}
         for t in range(PACK):
             diff = psum.tile([P, S // P, P], F32, name="bank%d" % (4 + t))
             for b in range(S // P):
                 cols = slice(b * P, (b + 1) * P)
                 nc.tensor.matmul(diff[:, b, :], fetched[t][:, cols], ident[:], start=True, stop=False, is_transpose=True)
                 nc.tensor.matmul(diff[:, b, :], minus_frame[t][:, cols], ident[:], start=False, stop=True, is_transpose=True)
-            size = ring.tile([P, S // P, P], F32, name="size")
+            size = keep.tile([P, S // P, P], F32, name="size%d" % t)
             nc.scalar.activation(size[:], diff[:], ACT.Abs)
-            back = psum.tile([P, S], F32, name="bank%d" % t)
-            for b in range(S // P):
+            sizes.append(size)
+            first = HEAD if t < ON_TENSOR else 0
+            back = psum.tile([P, S], F32, name="bank%d" % (t % 2))
+            for b in range(first // P, S // P):
                 nc.tensor.transpose(back[:, b * P : (b + 1) * P], size[:, b, :], ident[:])
             weighted = keep.tile([P, S], F32, name="dist%d" % t)
-            nc.scalar.activation(weighted[:], back[:], ACT.Copy, scale=gain[:, t : t + 1])
-            dist.append(weighted)
+            nc.scalar.activation(weighted[:, first:], back[:, first:], ACT.Copy, scale=gain[:, t : t + 1])
+            dist[t] = weighted
 
         z_head = keep.tile([P, PACK, HEAD], F32, name="z_head")
         z_tail = keep.tile([P, PACK, S - HEAD], F32, name="z_tail")
@@ -152,26 +162,52 @@ def tile_picked_dtwcell_none_p_kernel(tc, x_words, x_scales, w1, w2, w3, gs, off
 
         def cell(n, name):
             z4, lo, hi, t = steps[n]
-            if (n, name) == (6, "dk"):
+            if (n, name) == (6, "di"):
                 tile = keep.tile([P, hi - lo], F32, name="cell6", tag="woven0", align_bytes=64)
-            elif (n, name) == (7, "dj"):
+            elif (n, name) == (6, "dk"):
                 tile = keep.tile([P, hi - lo], F32, name="cell7", tag="woven256", align_bytes=64)
+            elif (n, name) == (0, "di"):
+                tile = keep.tile([P, hi - lo], F32, name="cell0", tag="dealt_w2", align_bytes=64)
+            elif (n, name) == (5, "di"):
+                tile = keep.tile([P, hi - lo], F32, name="cell5", tag="least3")
+            elif name == "dk":
+                tile = ring.tile([P, hi - lo], F32, name="cell_dk")
             else:
-                tile = ring.tile([P, hi - lo], F32, name="cell_" + name)
+                tile = keep.tile([P, hi - lo], F32, name="cell_" + name)
             gather(tile[:], cost[t], name, lo, hi)
             state[n, name] = tile
 
-        def least_of(n, first, second, result):
+        def pair(n):
             z4, lo, hi, t = steps[n]
-            tile = ring.tile([P, hi - lo], F32, name=result)
-            nc.vector.tensor_tensor(tile[:], state[n, first][:], state[n, second][:], ALU.min)
-            state[n, result] = tile
+            tile = ring.tile([P, hi - lo], F32, name="pair")
+            nc.vector.tensor_tensor(tile[:], state[n, "di"][:], state[n, "dj"][:], ALU.min)
+            state[n, "pair"] = tile
+
+        def least(n):
+            z4, lo, hi, t = steps[n]
+            tile = keep.tile([P, hi - lo], F32, name="least%d" % n, tag="least%d" % n)
+            nc.vector.tensor_tensor(tile[:], state[n, "pair"][:], state[n, "dk"][:], ALU.min)
+            state[n, "least"] = tile
 
         def weigh(n):
             z4, lo, hi, t = steps[n]
-            nc.vector.scalar_tensor_tensor(
-                z4[:, t, :], state[n, "least"][:], gain[:, t : t + 1], dist[t][:, lo:hi], ALU.mult, ALU.add
-            )
+            if n >= ON_TENSOR:
+                nc.vector.scalar_tensor_tensor(
+                    z4[:, t, :], state[n, "least"][:], gain[:, t : t + 1], dist[t][:, lo:hi], ALU.mult, ALU.add
+                )
+                return
+            blocks = HEAD // P
+            over = psum.tile([P, blocks, P], F32, name="bank1")
+            for b in range(blocks):
+                nc.tensor.transpose(over[:, b, :], state[n, "least"][:, b * P : (b + 1) * P], ident[:])
+            turned = ring.tile([P, blocks, P], F32, name="turned")
+            nc.scalar.copy(turned[:], over[:])
+            total = psum.tile([P, HEAD], F32, name="bank0")
+            for b in range(blocks):
+                cols = slice(b * P, (b + 1) * P)
+                nc.tensor.matmul(total[:, cols], sizes[t][:, b, :], ident[:], start=True, stop=False, is_transpose=True)
+                nc.tensor.matmul(total[:, cols], turned[:, b, :], ident[:], start=False, stop=True, is_transpose=True)
+            nc.scalar.activation(z4[:, t, :], total[:], ACT.Copy, scale=gain[:, t : t + 1])
 
         def quantise_z(z4, a, b, base, weave):
             woven = keep.tile([P, b - a, PACK], BF16, name="woven%d" % (base + a), tag="woven%d" % (base + a), align_bytes=64)
@@ -194,37 +230,47 @@ def tile_picked_dtwcell_none_p_kernel(tc, x_words, x_scales, w1, w2, w3, gs, off
             )
 
         def finish_head():
-            pieces = ((0, 256), (256, HEAD))
-            zq = [quantise_z(z_head, a, b, 0, nc.scalar.copy) for a, b in pieces]
-            result = keep.tile([P, C // P, HEAD], F32, name="result_head")
-            for blk in range(C // P):
-                acc = psum.tile([P, S], F32, name="bank%d" % (4 + blk))
-                for (a, b), piece in zip(pieces, zq):
-                    score(acc[:, a:b], blk, piece)
-                nc.scalar.activation(result[:, blk, :], acc[:, :HEAD], ACT.Copy, scale=OUT_SCALE)
-            nc.sync.dma_start(out[:, :HEAD].rearrange("(b p) j -> p b j", p=P), result[:])
+            bank = 4
+            for a, b in ((0, 256), (256, HEAD)):
+                zq = quantise_z(z_head, a, b, 0, nc.scalar.copy)
+                blocks = S // (b - a)
+                rows = out[:, a:b].rearrange("(h b p) j -> h p b j", b=blocks, p=P)
+                for h in range(C // P // blocks):
+                    acc = psum.tile([P, blocks, b - a], F32, name="bank%d" % bank)
+                    for i in range(blocks):
+                        score(acc[:, i, :], blocks * h + i, zq)
+                    result = keep.tile([P, blocks, b - a], F32, name="result_head%d" % bank)
+                    nc.scalar.activation(result[:], acc[:], ACT.Copy, scale=OUT_SCALE)
+                    nc.sync.dma_start(rows[h], result[:])
+                    bank = bank + 1
 
         def finish_tail():
             zq = quantise_z(z_tail, 0, S - HEAD, HEAD, nc.vector.tensor_copy)
-            result = keep.tile([P, C // P, S - HEAD], F32, name="result_tail")
-            acc = psum.tile([P, C // P, S - HEAD], F32, name="bank0")
-            for blk in range(C // P):
-                score(acc[:, blk, :], blk, zq)
-            nc.scalar.activation(result[:], acc[:], ACT.Copy, scale=OUT_SCALE)
-            nc.sync.dma_start(out[:, HEAD:].rearrange("(b p) j -> p b j", p=P), result[:])
+            rows = out[:, HEAD:].rearrange("(h b p) j -> h p b j", h=2, p=P)
+            for h in range(2):
+                result = keep.tile([P, 2, S - HEAD], F32, name="result_tail%d" % h)
+                acc = psum.tile([P, 2, S - HEAD], F32, name="bank%d" % (2 + h))
+                for b in range(2):
+                    score(acc[:, b, :], 2 * h + b, zq)
+                if h == 0:
+                    nc.scalar.activation(result[:], acc[:], ACT.Copy, scale=OUT_SCALE)
+                    nc.scalar.dma_start(rows[h], result[:])
+                else:
+                    nc.vector.tensor_scalar_mul(result[:], acc[:], OUT_SCALE)
+                    nc.sync.dma_start(rows[h], result[:])
 
         for n in range(len(steps)):
             cell(n, "di")
             cell(n, "dj")
             if n > 0:
-                least_of(n - 1, "pair", "dk", "least")
+                least(n - 1)
+            pair(n)
             cell(n, "dk")
-            least_of(n, "di", "dj", "pair")
             if n > 0:
                 weigh(n - 1)
             if n == PACK:
                 finish_head()
         last = len(steps) - 1
-        least_of(last, "pair", "dk", "least")
+        least(last)
         weigh(last)
         finish_tail()

@@ -37,9 +37,13 @@ def tile_picked_dtwcell_none_p_kernel(tc, x_words, x_scales, w1, w2, w3, gs, off
             return tile
 
         def load_weight(name, src):
-            raw = keep.tile([P, PACK, H], F32, name="raw_" + name)
-            nc.sync.dma_start(raw[:], src.rearrange("(p j) c -> p j c", j=PACK))
-            return raw
+            halves = []
+            for h in range(2):
+                tag = "raw_%s_%d" % (name, h)
+                half = keep.tile([P, PACK, H // 2], F32, name=tag, tag=tag, align_bytes=64)
+                nc.sync.dma_start(half[:], src[:, h * H // 2 : (h + 1) * H // 2].rearrange("(p j) c -> p j c", j=PACK))
+                halves.append(half)
+            return halves
 
         table_scales = keep.tile([P, T], U8, name="table_scales", align_bytes=64)
         nc.vector.memset(table_scales[:].bitcast(I32), 0)
@@ -80,10 +84,11 @@ def tile_picked_dtwcell_none_p_kernel(tc, x_words, x_scales, w1, w2, w3, gs, off
 
         def deal_weight(name):
             dealt = keep.tile([P, PACK, P, PACK], BF16, name="dealt_" + name, tag="dealt_" + name, align_bytes=64)
-            nc.scalar.copy(
-                dealt[:].rearrange("p t m j -> p m j t"),
-                raw[name][:].rearrange("p j (m t) -> p m j t", t=PACK),
-            )
+            for h in range(2):
+                nc.scalar.copy(
+                    dealt[:, :, h * P // 2 : (h + 1) * P // 2, :].rearrange("p t m j -> p m j t"),
+                    raw[name][h][:].rearrange("p j (m t) -> p m j t", t=PACK),
+                )
             return dealt
 
         def quantise_weight(name, dealt):
@@ -92,7 +97,7 @@ def tile_picked_dtwcell_none_p_kernel(tc, x_words, x_scales, w1, w2, w3, gs, off
             nc.vector.quantize_mx(codes[:].bitcast(FP8X4), scales[:], dealt[:].rearrange("p t m j -> p (t m j)"))
             return codes, scales
 
-        def project(weight, name, first_bank, result, sign):
+        def project(weight, name, first_bank, result, sign, spare=0):
             codes, scales = weight
             tiles = []
             for t in range(PACK):
@@ -107,8 +112,10 @@ def tile_picked_dtwcell_none_p_kernel(tc, x_words, x_scales, w1, w2, w3, gs, off
                     start=True,
                     stop=True,
                 )
-                tile = keep.tile([P, S], F32, name="%s%d" % (result, t))
-                nc.scalar.activation(tile[:], bank[:], ACT.Copy, scale=sign)
+                tile = keep.tile([P, S + spare], F32, name="%s%d" % (result, t))
+                if spare:
+                    nc.gpsimd.memset(tile[:, S:], 0.0)
+                nc.scalar.activation(tile[:, :S], bank[:], ACT.Copy, scale=sign)
                 tiles.append(tile)
             return tiles
 
@@ -121,18 +128,17 @@ def tile_picked_dtwcell_none_p_kernel(tc, x_words, x_scales, w1, w2, w3, gs, off
             pick_words(name, "words_" + name)
         for name in ("two", "cand"):
             pick_scales(name)
-        pick_words("cand", "words_cand")
         w3q = quantise_weight("w3", deal_weight("w3"))
-        ref = project(w3q, "thr", 0, "ref", 1.0)
+        pick_words("cand", "raw_w3_1")
+        ref = project(w3q, "thr", 0, "ref", 1.0, spare=S)
         pick_words("two", "dealt_w3")
         w1q = quantise_weight("w1", deal_weight("w1"))
-        dealt_w2 = deal_weight("w2")
         cost = project(w1q, "offs", 4, "cost", 1.0)
+        dealt_w2 = deal_weight("w2")
         fetched = []
         for t in range(PACK):
             tile = keep.tile([P, S], F32, name="fetched%d" % t, tag="dealt_w1" if t == 1 else "fetched%d" % t, align_bytes=64)
-            for lo in range(0, S, S // 2):
-                gather(tile[:, lo : lo + S // 2], ref[t], "col", lo, lo + S // 2)
+            gather(tile[:], ref[t], "col", 0, S)
             fetched.append(tile)
         w2q = quantise_weight("w2", dealt_w2)
         minus_frame = project(w2q, "two", 0, "minus_frame", -1.0)
@@ -160,32 +166,29 @@ def tile_picked_dtwcell_none_p_kernel(tc, x_words, x_scales, w1, w2, w3, gs, off
         steps = [(z_head, 0, HEAD, t) for t in range(PACK)] + [(z_tail, HEAD, S, t) for t in range(PACK)]
         state = {}
 
+        inherits = {(0, "dj"): "dealt_w2", (5, "di"): "least3", (6, "di"): "woven0", (6, "dk"): "woven256"}
+
+        def step_tile(n, name):
+            z4, lo, hi, t = steps[n]
+            if (n, name) in inherits:
+                tile = keep.tile([P, hi - lo], F32, name="%s%d" % (name, n), tag=inherits[n, name], align_bytes=64)
+            elif name in ("dk", "pair"):
+                tile = ring.tile([P, hi - lo], F32, name="step_" + name)
+            else:
+                tile = keep.tile([P, hi - lo], F32, name="step_" + name)
+            state[n, name] = tile
+            return tile
+
         def cell(n, name):
             z4, lo, hi, t = steps[n]
-            if (n, name) == (6, "di"):
-                tile = keep.tile([P, hi - lo], F32, name="cell6", tag="woven0", align_bytes=64)
-            elif (n, name) == (6, "dk"):
-                tile = keep.tile([P, hi - lo], F32, name="cell7", tag="woven256", align_bytes=64)
-            elif (n, name) == (0, "di"):
-                tile = keep.tile([P, hi - lo], F32, name="cell0", tag="dealt_w2", align_bytes=64)
-            elif (n, name) == (5, "di"):
-                tile = keep.tile([P, hi - lo], F32, name="cell5", tag="least3")
-            elif name == "dk":
-                tile = ring.tile([P, hi - lo], F32, name="cell_dk")
-            else:
-                tile = keep.tile([P, hi - lo], F32, name="cell_" + name)
-            gather(tile[:], cost[t], name, lo, hi)
-            state[n, name] = tile
+            gather(step_tile(n, name)[:], cost[t], name, lo, hi)
 
         def pair(n):
-            z4, lo, hi, t = steps[n]
-            tile = ring.tile([P, hi - lo], F32, name="pair")
-            nc.vector.tensor_tensor(tile[:], state[n, "di"][:], state[n, "dj"][:], ALU.min)
-            state[n, "pair"] = tile
+            nc.vector.tensor_tensor(step_tile(n, "pair")[:], state[n, "di"][:], state[n, "dj"][:], ALU.min)
 
         def least(n):
             z4, lo, hi, t = steps[n]
-            tile = keep.tile([P, hi - lo], F32, name="least%d" % n, tag="least%d" % n)
+            tile = keep.tile([P, hi - lo], F32, name="least%d" % n, tag="least%d" % n, align_bytes=64)
             nc.vector.tensor_tensor(tile[:], state[n, "pair"][:], state[n, "dk"][:], ALU.min)
             state[n, "least"] = tile
 
@@ -211,7 +214,10 @@ def tile_picked_dtwcell_none_p_kernel(tc, x_words, x_scales, w1, w2, w3, gs, off
 
         def quantise_z(z4, a, b, base, weave):
             woven = keep.tile([P, b - a, PACK], BF16, name="woven%d" % (base + a), tag="woven%d" % (base + a), align_bytes=64)
-            weave(woven[:], z4[:, :, a:b].rearrange("p t j -> p j t"))
+            weave(
+                woven[:].rearrange("p (c i) t -> p c t i", i=PACK),
+                z4[:, :, a:b].rearrange("p t (c i) -> p c t i", i=PACK),
+            )
             codes = keep.tile([P, b - a], U32, name="zcodes%d" % (base + a), align_bytes=64)
             scales = keep.tile([P, b - a], U8, name="zscales%d" % (base + a), align_bytes=64)
             nc.vector.quantize_mx(codes[:].bitcast(FP8X4), scales[:], woven[:].rearrange("p j t -> p (j t)"))

@@ -53,15 +53,15 @@ def tile_picked_dtwcell_none_p_kernel(tc, x_words, x_scales, w1, w2, w3, gs, off
                 x_scales[0, 4 * q : 4 * q + 4, :].bitcast(I32),
             )
         lists = {}
-        for name, src in (("thr", thr), ("offs", offs)):
+        for name, src in (("thr", thr), ("offs", offs), ("two", two)):
             lists[name] = load_list(name, src)
         table_words = keep.tile([P, T], I32, name="table_words", align_bytes=64)
         nc.sync.dma_start(table_words[:], x_words[0].rearrange("p n r -> p (n r)").bitcast(I32))
+        lists["cand"] = load_list("cand", cand)
         raw = {"w3": load_weight("w3", w3)}
-        for name, src in (("two", two), ("cand", cand)):
-            lists[name] = load_list(name, src)
+        lists["col"] = load_list("col", col)
         raw["w1"] = load_weight("w1", w1)
-        for name, src in (("col", col), ("di", di), ("dj", dj), ("dk", dk)):
+        for name, src in (("di", di), ("dj", dj), ("dk", dk)):
             lists[name] = load_list(name, src)
         gain = keep.tile([P, PACK], F32, name="gain")
         nc.sync.dma_start(gain[:], gs.rearrange("(p t) o -> p (t o)", t=PACK))
@@ -114,7 +114,7 @@ def tile_picked_dtwcell_none_p_kernel(tc, x_words, x_scales, w1, w2, w3, gs, off
                 )
                 tile = keep.tile([P, S + spare], F32, name="%s%d" % (result, t))
                 if spare:
-                    nc.gpsimd.memset(tile[:, S:], 0.0)
+                    nc.vector.memset(tile[:, S:], 0.0)
                 nc.scalar.activation(tile[:, :S], bank[:], ACT.Copy, scale=sign)
                 tiles.append(tile)
             return tiles
@@ -122,12 +122,11 @@ def tile_picked_dtwcell_none_p_kernel(tc, x_words, x_scales, w1, w2, w3, gs, off
         def gather(dst, window, name, lo, hi):
             nc.vector.tensor_copy(dst, window[:].indirect(lists[name][:, lo // STRIPE : hi // STRIPE]))
 
-        for name in ("thr", "offs"):
+        for name in ("thr", "offs", "two"):
             pick_scales(name)
         for name in ("thr", "offs"):
             pick_words(name, "words_" + name)
-        for name in ("two", "cand"):
-            pick_scales(name)
+        pick_scales("cand")
         w3q = quantise_weight("w3", deal_weight("w3"))
         pick_words("cand", "raw_w3_1")
         ref = project(w3q, "thr", 0, "ref", 1.0, spare=S)

@@ -19,9 +19,12 @@ ACT = mybir.ActivationFunctionType
 P = 128
 PACK = 4
 STRIPE = 16
-HEAD = 384
-ON_TENSOR = 3
+QUADRANT = 32
 OUT_SCALE = 0.0625
+HEAD = 384
+HEAD_PIECES = ((0, 256), (256, HEAD))
+WHOLE = 2
+ON_TENSOR = 3
 
 
 def tile_picked_dtwcell_none_p_kernel(tc, x_words, x_scales, w1, w2, w3, gs, offs, two, thr, di, dj, dk, col, cand, out):
@@ -31,10 +34,14 @@ def tile_picked_dtwcell_none_p_kernel(tc, x_words, x_scales, w1, w2, w3, gs, off
         ring = ctx.enter_context(tc.tile_pool(name="ring", bufs=2))
         psum = ctx.enter_context(tc.psum_pool(name="psum", bufs=1))
 
+        def bank_tile(number, shape):
+            return psum.tile(shape, F32, name="bank%d" % number)
+
+        lists = {}
+
         def load_list(name, src):
-            tile = keep.tile([P, S // STRIPE], U16, name="list_" + name)
-            nc.sync.dma_start(tile[:], src)
-            return tile
+            lists[name] = keep.tile([P, S // STRIPE], U16, name="list_" + name)
+            nc.sync.dma_start(lists[name][:], src)
 
         def load_weight(name, src):
             halves = []
@@ -47,22 +54,21 @@ def tile_picked_dtwcell_none_p_kernel(tc, x_words, x_scales, w1, w2, w3, gs, off
 
         table_scales = keep.tile([P, T], U8, name="table_scales", align_bytes=64)
         nc.vector.memset(table_scales[:].bitcast(I32), 0)
-        for q in range(4):
+        for q in range(P // QUADRANT):
             nc.sync.dma_start(
-                table_scales[32 * q : 32 * q + 4, :].bitcast(I32),
-                x_scales[0, 4 * q : 4 * q + 4, :].bitcast(I32),
+                table_scales[QUADRANT * q : QUADRANT * q + PACK, :].bitcast(I32),
+                x_scales[0, PACK * q : PACK * q + PACK, :].bitcast(I32),
             )
-        lists = {}
         for name, src in (("thr", thr), ("offs", offs), ("two", two)):
-            lists[name] = load_list(name, src)
+            load_list(name, src)
         table_words = keep.tile([P, T], I32, name="table_words", align_bytes=64)
         nc.sync.dma_start(table_words[:], x_words[0].rearrange("p n r -> p (n r)").bitcast(I32))
-        lists["cand"] = load_list("cand", cand)
+        load_list("cand", cand)
         raw = {"w3": load_weight("w3", w3)}
-        lists["col"] = load_list("col", col)
+        load_list("col", col)
         raw["w1"] = load_weight("w1", w1)
         for name, src in (("di", di), ("dj", dj), ("dk", dk)):
-            lists[name] = load_list(name, src)
+            load_list(name, src)
         gain = keep.tile([P, PACK], F32, name="gain")
         nc.sync.dma_start(gain[:], gs.rearrange("(p t) o -> p (t o)", t=PACK))
         raw["w2"] = load_weight("w2", w2)
@@ -73,14 +79,12 @@ def tile_picked_dtwcell_none_p_kernel(tc, x_words, x_scales, w1, w2, w3, gs, off
         picked_scales, picked_words = {}, {}
 
         def pick_scales(name):
-            tile = keep.tile([P, S], U8, name="scales_" + name, align_bytes=64)
-            nc.vector.tensor_copy(tile[:], table_scales[:].indirect(lists[name][:]))
-            picked_scales[name] = tile
+            picked_scales[name] = keep.tile([P, S], U8, name="scales_" + name, align_bytes=64)
+            nc.vector.tensor_copy(picked_scales[name][:], table_scales[:].indirect(lists[name][:]))
 
-        def pick_words(name, slot):
-            tile = keep.tile([P, S], U32, name="words_" + name, tag=slot, align_bytes=64)
-            nc.vector.tensor_copy(tile[:], table_words[:].bitcast(U32).indirect(lists[name][:]))
-            picked_words[name] = tile
+        def pick_words(name, tag):
+            picked_words[name] = keep.tile([P, S], U32, name="words_" + name, tag=tag, align_bytes=64)
+            nc.vector.tensor_copy(picked_words[name][:], table_words[:].bitcast(U32).indirect(lists[name][:]))
 
         def deal_weight(name):
             dealt = keep.tile([P, PACK, P, PACK], BF16, name="dealt_" + name, tag="dealt_" + name, align_bytes=64)
@@ -97,14 +101,14 @@ def tile_picked_dtwcell_none_p_kernel(tc, x_words, x_scales, w1, w2, w3, gs, off
             nc.vector.quantize_mx(codes[:].bitcast(FP8X4), scales[:], dealt[:].rearrange("p t m j -> p (t m j)"))
             return codes, scales
 
-        def project(weight, name, first_bank, result, sign, spare=0):
+        def project(weight, name, first_bank, result, sign, wide, zeroing):
             codes, scales = weight
-            tiles = []
+            planes = []
             for t in range(PACK):
-                bank = psum.tile([P, S], F32, name="bank%d" % (first_bank + t))
+                acc = bank_tile(first_bank + t, [P, S])
                 cols = slice(t * P, (t + 1) * P)
                 nc.tensor.matmul_mx(
-                    out=bank[:],
+                    out=acc[:],
                     lhsT=codes[:, cols].bitcast(FP8X4),
                     lhsT_scale=scales[:, cols],
                     rhs=picked_words[name][:].bitcast(FP8X4),
@@ -112,15 +116,15 @@ def tile_picked_dtwcell_none_p_kernel(tc, x_words, x_scales, w1, w2, w3, gs, off
                     start=True,
                     stop=True,
                 )
-                tile = keep.tile([P, S + spare], F32, name="%s%d" % (result, t))
-                if spare:
-                    nc.vector.memset(tile[:, S:], 0.0)
-                nc.scalar.activation(tile[:, :S], bank[:], ACT.Copy, scale=sign)
-                tiles.append(tile)
-            return tiles
+                plane = keep.tile([P, 2 * S if t < wide else S], F32, name="%s%d" % (result, t))
+                if t < wide:
+                    zeroing.memset(plane[:, S:], 0.0)
+                nc.scalar.activation(plane[:, :S], acc[:], ACT.Copy, scale=sign)
+                planes.append(plane)
+            return planes
 
-        def gather(dst, window, name, lo, hi):
-            nc.vector.tensor_copy(dst, window[:].indirect(lists[name][:, lo // STRIPE : hi // STRIPE]))
+        def gather(dst, plane, name, lo, hi):
+            nc.vector.tensor_copy(dst, plane[:].indirect(lists[name][:, lo // STRIPE : hi // STRIPE]))
 
         for name in ("thr", "offs", "two"):
             pick_scales(name)
@@ -129,101 +133,103 @@ def tile_picked_dtwcell_none_p_kernel(tc, x_words, x_scales, w1, w2, w3, gs, off
         pick_scales("cand")
         w3q = quantise_weight("w3", deal_weight("w3"))
         pick_words("cand", "raw_w3_1")
-        ref = project(w3q, "thr", 0, "ref", 1.0, spare=S)
+        ref = project(w3q, "thr", 0, "ref", 1.0, PACK, nc.vector)
         pick_words("two", "dealt_w3")
         w1q = quantise_weight("w1", deal_weight("w1"))
-        cost = project(w1q, "offs", 4, "cost", 1.0)
         dealt_w2 = deal_weight("w2")
+        cost = project(w1q, "offs", 4, "cost", 1.0, WHOLE, nc.gpsimd)
         fetched = []
         for t in range(PACK):
-            tile = keep.tile([P, S], F32, name="fetched%d" % t, tag="dealt_w1" if t == 1 else "fetched%d" % t, align_bytes=64)
-            gather(tile[:], ref[t], "col", 0, S)
-            fetched.append(tile)
+            tag = "dealt_w1" if t == 1 else "fetched%d" % t
+            fetched.append(keep.tile([P, S], F32, name="fetched%d" % t, tag=tag, align_bytes=64))
+            gather(fetched[t][:], ref[t], "col", 0, S)
         w2q = quantise_weight("w2", dealt_w2)
-        minus_frame = project(w2q, "two", 0, "minus_frame", -1.0)
+        minus_frame = project(w2q, "two", 0, "minus_frame", -1.0, 0, None)
 
-        sizes, dist = [], {}
+        def add_transposes(dst, first, second):
+            nc.tensor.matmul(dst, first, ident[:], start=True, stop=False, is_transpose=True)
+            nc.tensor.matmul(dst, second, ident[:], start=False, stop=True, is_transpose=True)
+
+        turned_dist, weighted_dist = [], {}
         for t in range(PACK):
-            diff = psum.tile([P, S // P, P], F32, name="bank%d" % (4 + t))
+            diff = bank_tile(4 + t, [P, S // P, P])
             for b in range(S // P):
                 cols = slice(b * P, (b + 1) * P)
-                nc.tensor.matmul(diff[:, b, :], fetched[t][:, cols], ident[:], start=True, stop=False, is_transpose=True)
-                nc.tensor.matmul(diff[:, b, :], minus_frame[t][:, cols], ident[:], start=False, stop=True, is_transpose=True)
-            size = keep.tile([P, S // P, P], F32, name="size%d" % t)
-            nc.scalar.activation(size[:], diff[:], ACT.Abs)
-            sizes.append(size)
+                add_transposes(diff[:, b, :], fetched[t][:, cols], minus_frame[t][:, cols])
+            turned_dist.append(keep.tile([P, S // P, P], F32, name="turned_dist%d" % t))
+            nc.scalar.activation(turned_dist[t][:], diff[:], ACT.Abs)
+            if t < WHOLE:
+                continue
             first = HEAD if t < ON_TENSOR else 0
-            back = psum.tile([P, S], F32, name="bank%d" % (t % 2))
+            back = bank_tile(t - WHOLE, [P, S])
             for b in range(first // P, S // P):
-                nc.tensor.transpose(back[:, b * P : (b + 1) * P], size[:, b, :], ident[:])
-            weighted = keep.tile([P, S], F32, name="dist%d" % t)
-            nc.scalar.activation(weighted[:, first:], back[:, first:], ACT.Copy, scale=gain[:, t : t + 1])
-            dist[t] = weighted
+                nc.tensor.transpose(back[:, b * P : (b + 1) * P], turned_dist[t][:, b, :], ident[:])
+            weighted_dist[t] = keep.tile([P, S], F32, name="weighted_dist%d" % t)
+            nc.scalar.activation(weighted_dist[t][:, first:], back[:, first:], ACT.Copy, scale=gain[:, t : t + 1])
 
         z_head = keep.tile([P, PACK, HEAD], F32, name="z_head")
         z_tail = keep.tile([P, PACK, S - HEAD], F32, name="z_tail")
-        steps = [(z_head, 0, HEAD, t) for t in range(PACK)] + [(z_tail, HEAD, S, t) for t in range(PACK)]
-        state = {}
-
-        inherits = {(0, "dj"): "dealt_w2", (5, "di"): "least3", (6, "di"): "woven0", (6, "dk"): "woven256"}
+        steps = [(t, 0, S if t < WHOLE else HEAD) for t in range(PACK)] + [(t, HEAD, S) for t in range(WHOLE, PACK)]
+        first_tail, last = PACK, len(steps) - 1
+        made = {}
+        inherits = {(0, "di"): "dealt_w2", (first_tail, "pair"): "least%d" % (first_tail - 1), (last, "dk"): "woven0"}
 
         def step_tile(n, name):
-            z4, lo, hi, t = steps[n]
+            t, lo, hi = steps[n]
             if (n, name) in inherits:
-                tile = keep.tile([P, hi - lo], F32, name="%s%d" % (name, n), tag=inherits[n, name], align_bytes=64)
-            elif name in ("dk", "pair"):
-                tile = ring.tile([P, hi - lo], F32, name="step_" + name)
+                made[n, name] = keep.tile(
+                    [P, hi - lo], F32, name="%s%d" % (name, n), tag=inherits[n, name], align_bytes=64
+                )
             else:
-                tile = keep.tile([P, hi - lo], F32, name="step_" + name)
-            state[n, name] = tile
-            return tile
+                made[n, name] = keep.tile([P, hi - lo], F32, name="%s%d" % (name, n))
+            return made[n, name]
 
         def cell(n, name):
-            z4, lo, hi, t = steps[n]
+            t, lo, hi = steps[n]
             gather(step_tile(n, name)[:], cost[t], name, lo, hi)
 
         def pair(n):
-            nc.vector.tensor_tensor(step_tile(n, "pair")[:], state[n, "di"][:], state[n, "dj"][:], ALU.min)
+            nc.vector.tensor_tensor(step_tile(n, "pair")[:], made[n, "di"][:], made[n, "dj"][:], ALU.min)
 
         def least(n):
-            z4, lo, hi, t = steps[n]
-            tile = keep.tile([P, hi - lo], F32, name="least%d" % n, tag="least%d" % n, align_bytes=64)
-            nc.vector.tensor_tensor(tile[:], state[n, "pair"][:], state[n, "dk"][:], ALU.min)
-            state[n, "least"] = tile
+            t, lo, hi = steps[n]
+            made[n, "least"] = keep.tile([P, hi - lo], F32, name="least%d" % n, tag="least%d" % n, align_bytes=64)
+            nc.vector.tensor_tensor(made[n, "least"][:], made[n, "pair"][:], made[n, "dk"][:], ALU.min)
 
         def weigh(n):
-            z4, lo, hi, t = steps[n]
+            t, lo, hi = steps[n]
             if n >= ON_TENSOR:
+                z_part = z_head if lo == 0 else z_tail
                 nc.vector.scalar_tensor_tensor(
-                    z4[:, t, :], state[n, "least"][:], gain[:, t : t + 1], dist[t][:, lo:hi], ALU.mult, ALU.add
+                    z_part[:, t, :], made[n, "least"][:], gain[:, t : t + 1], weighted_dist[t][:, lo:hi], ALU.mult, ALU.add
                 )
                 return
-            blocks = HEAD // P
-            over = psum.tile([P, blocks, P], F32, name="bank1")
+            blocks = hi // P
+            over = bank_tile((7, 1)[n % 2], [P, blocks, P])
             for b in range(blocks):
-                nc.tensor.transpose(over[:, b, :], state[n, "least"][:, b * P : (b + 1) * P], ident[:])
-            turned = ring.tile([P, blocks, P], F32, name="turned")
-            nc.scalar.copy(turned[:], over[:])
-            total = psum.tile([P, HEAD], F32, name="bank0")
+                nc.tensor.transpose(over[:, b, :], made[n, "least"][:, b * P : (b + 1) * P], ident[:])
+            turned_least = ring.tile([P, blocks, P], F32, name="turned_least")
+            nc.scalar.copy(turned_least[:], over[:])
+            total = bank_tile((0, 6)[n % 2], [P, hi])
             for b in range(blocks):
-                cols = slice(b * P, (b + 1) * P)
-                nc.tensor.matmul(total[:, cols], sizes[t][:, b, :], ident[:], start=True, stop=False, is_transpose=True)
-                nc.tensor.matmul(total[:, cols], turned[:, b, :], ident[:], start=False, stop=True, is_transpose=True)
-            nc.scalar.activation(z4[:, t, :], total[:], ACT.Copy, scale=gain[:, t : t + 1])
+                add_transposes(total[:, b * P : (b + 1) * P], turned_dist[t][:, b, :], turned_least[:, b, :])
+            nc.scalar.activation(z_head[:, t, :], total[:, :HEAD], ACT.Copy, scale=gain[:, t : t + 1])
+            if hi > HEAD:
+                nc.scalar.activation(z_tail[:, t, :], total[:, HEAD:], ACT.Copy, scale=gain[:, t : t + 1])
 
-        def quantise_z(z4, a, b, base, weave):
-            woven = keep.tile([P, b - a, PACK], BF16, name="woven%d" % (base + a), tag="woven%d" % (base + a), align_bytes=64)
+        def quantise_z(z_part, a, b, first_column, weave, tag):
+            woven = keep.tile([P, b - a, PACK], BF16, name="woven%d" % first_column, tag=tag, align_bytes=64)
             weave(
                 woven[:].rearrange("p (c i) t -> p c t i", i=PACK),
-                z4[:, :, a:b].rearrange("p t (c i) -> p c t i", i=PACK),
+                z_part[:, :, a:b].rearrange("p t (c i) -> p c t i", i=PACK),
             )
-            codes = keep.tile([P, b - a], U32, name="zcodes%d" % (base + a), align_bytes=64)
-            scales = keep.tile([P, b - a], U8, name="zscales%d" % (base + a), align_bytes=64)
+            codes = keep.tile([P, b - a], U32, name="zcodes%d" % first_column, align_bytes=64)
+            scales = keep.tile([P, b - a], U8, name="zscales%d" % first_column, align_bytes=64)
             nc.vector.quantize_mx(codes[:].bitcast(FP8X4), scales[:], woven[:].rearrange("p j t -> p (j t)"))
             return codes, scales
 
-        def score(acc, blk, zq):
-            rows = slice(blk * P, (blk + 1) * P)
+        def score(acc, block, zq):
+            rows = slice(block * P, (block + 1) * P)
             nc.tensor.matmul_mx(
                 out=acc,
                 lhsT=picked_words["cand"][:, rows].bitcast(FP8X4),
@@ -235,26 +241,26 @@ def tile_picked_dtwcell_none_p_kernel(tc, x_words, x_scales, w1, w2, w3, gs, off
             )
 
         def finish_head():
-            bank = 4
-            for a, b in ((0, 256), (256, HEAD)):
-                zq = quantise_z(z_head, a, b, 0, nc.scalar.copy)
+            number = 4
+            for a, b in HEAD_PIECES:
+                zq = quantise_z(z_head, a, b, a, nc.scalar.copy, "woven%d" % a)
                 blocks = S // (b - a)
                 rows = out[:, a:b].rearrange("(h b p) j -> h p b j", b=blocks, p=P)
                 for h in range(C // P // blocks):
-                    acc = psum.tile([P, blocks, b - a], F32, name="bank%d" % bank)
+                    acc = bank_tile(number, [P, blocks, b - a])
                     for i in range(blocks):
                         score(acc[:, i, :], blocks * h + i, zq)
-                    result = keep.tile([P, blocks, b - a], F32, name="result_head%d" % bank)
+                    result = keep.tile([P, blocks, b - a], F32, name="result_head%d" % number)
                     nc.scalar.activation(result[:], acc[:], ACT.Copy, scale=OUT_SCALE)
                     nc.sync.dma_start(rows[h], result[:])
-                    bank = bank + 1
+                    number = number + 1
 
         def finish_tail():
-            zq = quantise_z(z_tail, 0, S - HEAD, HEAD, nc.vector.tensor_copy)
+            zq = quantise_z(z_tail, 0, S - HEAD, HEAD, nc.vector.tensor_copy, "woven%d" % HEAD_PIECES[-1][0])
             rows = out[:, HEAD:].rearrange("(h b p) j -> h p b j", h=2, p=P)
             for h in range(2):
                 result = keep.tile([P, 2, S - HEAD], F32, name="result_tail%d" % h)
-                acc = psum.tile([P, 2, S - HEAD], F32, name="bank%d" % (2 + h))
+                acc = bank_tile(2 + h, [P, 2, S - HEAD])
                 for b in range(2):
                     score(acc[:, b, :], 2 * h + b, zq)
                 if h == 0:
@@ -264,18 +270,23 @@ def tile_picked_dtwcell_none_p_kernel(tc, x_words, x_scales, w1, w2, w3, gs, off
                     nc.vector.tensor_scalar_mul(result[:], acc[:], OUT_SCALE)
                     nc.sync.dma_start(rows[h], result[:])
 
-        for n in range(len(steps)):
+        for n in range(last):
             cell(n, "di")
-            cell(n, "dj")
             if n > 0:
                 least(n - 1)
-            pair(n)
-            cell(n, "dk")
+            cell(n, "dj")
             if n > 0:
                 weigh(n - 1)
-            if n == PACK:
+            if n == first_tail:
                 finish_head()
-        last = len(steps) - 1
+            cell(n, "dk")
+            pair(n)
+        cell(last, "di")
+        cell(last, "dj")
+        least(last - 1)
+        pair(last)
+        cell(last, "dk")
+        weigh(last - 1)
         least(last)
         weigh(last)
         finish_tail()

from contextlib import ExitStack

import concourse.mybir as mybir
from concourse.masks import make_identity

K, T, S, H, C = 512, 2048, 512, 512, 512
FLOPS = 2 * K * (3 * H * S + C * S)

F32 = mybir.dt.float32
BF16 = mybir.dt.bfloat16
I32 = mybir.dt.int32
U32 = mybir.dt.uint32
U16 = mybir.dt.uint16
U8 = mybir.dt.uint8
FP8X4 = mybir.dt.float8_e4m3fn_x4
ALU = mybir.AluOpType
ACT = mybir.ActivationFunctionType

P = 128
PACK = 4
STRIPE = 16
QUADRANT = 32
OUT_SCALE = 0.0625
HEAD = 384
HEAD_PIECES = ((0, 256), (256, HEAD))
WHOLE = 2
ON_TENSOR = 3


def tile_picked_dtwcell_none_p_kernel(tc, x_words, x_scales, w1, w2, w3, gs, offs, two, thr, di, dj, dk, col, cand, out):
    nc = tc.nc
    with ExitStack() as ctx:
        keep = ctx.enter_context(tc.tile_pool(name="keep", bufs=1))
        ring = ctx.enter_context(tc.tile_pool(name="ring", bufs=2))
        psum = ctx.enter_context(tc.psum_pool(name="psum", bufs=1))

        def bank_tile(number, shape):
            return psum.tile(shape, F32, name="bank%d" % number)

        lists = {}

        def load_list(name, src):
            lists[name] = keep.tile([P, S // STRIPE], U16, name="list_" + name)
            nc.sync.dma_start(lists[name][:], src)

        def load_weight(name, src):
            halves = []
            for h in range(2):
                tag = "raw_%s_%d" % (name, h)
                half = keep.tile([P, PACK, H // 2], F32, name=tag, tag=tag, align_bytes=64)
                nc.sync.dma_start(half[:], src[:, h * H // 2 : (h + 1) * H // 2].rearrange("(p j) c -> p j c", j=PACK))
                halves.append(half)
            return halves

        table_scales = keep.tile([P, T], U8, name="table_scales", align_bytes=64)
        nc.vector.memset(table_scales[:].bitcast(I32), 0)
        for q in range(P // QUADRANT):
            nc.sync.dma_start(
                table_scales[QUADRANT * q : QUADRANT * q + PACK, :].bitcast(I32),
                x_scales[0, PACK * q : PACK * q + PACK, :].bitcast(I32),
            )
        for name, src in (("thr", thr), ("offs", offs), ("two", two)):
            load_list(name, src)
        table_words = keep.tile([P, T], I32, name="table_words", align_bytes=64)
        nc.sync.dma_start(table_words[:], x_words[0].rearrange("p n r -> p (n r)").bitcast(I32))
        load_list("cand", cand)
        raw = {"w3": load_weight("w3", w3)}
        load_list("col", col)
        raw["w1"] = load_weight("w1", w1)
        for name, src in (("di", di), ("dj", dj), ("dk", dk)):
            load_list(name, src)
        gain = keep.tile([P, PACK], F32, name="gain")
        nc.sync.dma_start(gain[:], gs.rearrange("(p t) o -> p (t o)", t=PACK))
        raw["w2"] = load_weight("w2", w2)

        ident = keep.tile([P, P], F32, name="ident")
        make_identity(nc, ident[:])

        picked_scales, picked_words = {}, {}

        def pick_scales(name):
            picked_scales[name] = keep.tile([P, S], U8, name="scales_" + name, align_bytes=64)
            nc.vector.tensor_copy(picked_scales[name][:], table_scales[:].indirect(lists[name][:]))

        def pick_words(name, tag):
            picked_words[name] = keep.tile([P, S], U32, name="words_" + name, tag=tag, align_bytes=64)
            nc.vector.tensor_copy(picked_words[name][:], table_words[:].bitcast(U32).indirect(lists[name][:]))

        def deal_weight(name):
            dealt = keep.tile([P, PACK, P, PACK], BF16, name="dealt_" + name, tag="dealt_" + name, align_bytes=64)
            for h in range(2):
                nc.scalar.copy(
                    dealt[:, :, h * P // 2 : (h + 1) * P // 2, :].rearrange("p t m j -> p m j t"),
                    raw[name][h][:].rearrange("p j (m t) -> p m j t", t=PACK),
                )
            return dealt

        def quantise_weight(name, dealt):
            codes = keep.tile([P, H], U32, name="codes_" + name, align_bytes=64)
            scales = keep.tile([P, H], U8, name="wscales_" + name, align_bytes=64)
            nc.vector.quantize_mx(codes[:].bitcast(FP8X4), scales[:], dealt[:].rearrange("p t m j -> p (t m j)"))
            return codes, scales

        def project(weight, name, first_bank, result, sign, wide, zeroing):
            codes, scales = weight
            planes = []
            for t in range(PACK):
                acc = bank_tile(first_bank + t, [P, S])
                cols = slice(t * P, (t + 1) * P)
                nc.tensor.matmul_mx(
                    out=acc[:],
                    lhsT=codes[:, cols].bitcast(FP8X4),
                    lhsT_scale=scales[:, cols],
                    rhs=picked_words[name][:].bitcast(FP8X4),
                    rhs_scale=picked_scales[name][:],
                    start=True,
                    stop=True,
                )
                plane = keep.tile([P, 2 * S if t < wide else S], F32, name="%s%d" % (result, t))
                if t < wide:
                    zeroing.memset(plane[:, S:], 0.0)
                nc.scalar.activation(plane[:, :S], acc[:], ACT.Copy, scale=sign)
                planes.append(plane)
            return planes

        def gather(dst, plane, name, lo, hi):
            nc.vector.tensor_copy(dst, plane[:].indirect(lists[name][:, lo // STRIPE : hi // STRIPE]))

        for name in ("thr", "offs", "two"):
            pick_scales(name)
        for name in ("thr", "offs"):
            pick_words(name, "words_" + name)
        pick_scales("cand")
        w3q = quantise_weight("w3", deal_weight("w3"))
        pick_words("cand", "raw_w3_1")
        ref = project(w3q, "thr", 0, "ref", 1.0, PACK, nc.vector)
        pick_words("two", "dealt_w3")
        w1q = quantise_weight("w1", deal_weight("w1"))
        dealt_w2 = deal_weight("w2")
        cost = project(w1q, "offs", 4, "cost", 1.0, WHOLE, nc.gpsimd)
        fetched = []
        for t in range(PACK):
            tag = "dealt_w1" if t == 1 else "fetched%d" % t
            fetched.append(keep.tile([P, S], F32, name="fetched%d" % t, tag=tag, align_bytes=64))
            gather(fetched[t][:], ref[t], "col", 0, S)
        w2q = quantise_weight("w2", dealt_w2)
        minus_frame = project(w2q, "two", 0, "minus_frame", -1.0, 0, None)

        def add_transposes(dst, first, second):
            nc.tensor.matmul(dst, first, ident[:], start=True, stop=False, is_transpose=True)
            nc.tensor.matmul(dst, second, ident[:], start=False, stop=True, is_transpose=True)

        turned_dist, weighted_dist = [], {}
        for t in range(PACK):
            diff = bank_tile(4 + t, [P, S // P, P])
            for b in range(S // P):
                cols = slice(b * P, (b + 1) * P)
                add_transposes(diff[:, b, :], fetched[t][:, cols], minus_frame[t][:, cols])
            turned_dist.append(keep.tile([P, S // P, P], F32, name="turned_dist%d" % t))
            nc.scalar.activation(turned_dist[t][:], diff[:], ACT.Abs)
            if t < WHOLE:
                continue
            first = HEAD if t < ON_TENSOR else 0
            back = bank_tile(t - WHOLE, [P, S])
            for b in range(first // P, S // P):
                nc.tensor.transpose(back[:, b * P : (b + 1) * P], turned_dist[t][:, b, :], ident[:])
            weighted_dist[t] = keep.tile([P, S], F32, name="weighted_dist%d" % t)
            nc.scalar.activation(weighted_dist[t][:, first:], back[:, first:], ACT.Copy, scale=gain[:, t : t + 1])

        z_head = keep.tile([P, PACK, HEAD], F32, name="z_head")
        z_tail = keep.tile([P, PACK, S - HEAD], F32, name="z_tail")
        steps = [(t, 0, S if t < WHOLE else HEAD) for t in range(PACK)] + [(t, HEAD, S) for t in range(WHOLE, PACK)]
        first_tail, last = PACK, len(steps) - 1
        made = {}
        inherits = {(0, "di"): "dealt_w2", (first_tail, "pair"): "least%d" % (first_tail - 1), (last, "dk"): "woven0"}

        def step_tile(n, name):
            t, lo, hi = steps[n]
            if (n, name) in inherits:
                made[n, name] = keep.tile(
                    [P, hi - lo], F32, name="%s%d" % (name, n), tag=inherits[n, name], align_bytes=64
                )
            else:
                made[n, name] = keep.tile([P, hi - lo], F32, name="%s%d" % (name, n))
            return made[n, name]

        def cell(n, name):
            t, lo, hi = steps[n]
            gather(step_tile(n, name)[:], cost[t], name, lo, hi)

        def pair(n):
            nc.vector.tensor_tensor(step_tile(n, "pair")[:], made[n, "di"][:], made[n, "dj"][:], ALU.min)

        def least(n):
            t, lo, hi = steps[n]
            made[n, "least"] = keep.tile([P, hi - lo], F32, name="least%d" % n, tag="least%d" % n, align_bytes=64)
            nc.vector.tensor_tensor(made[n, "least"][:], made[n, "pair"][:], made[n, "dk"][:], ALU.min)

        def weigh(n):
            t, lo, hi = steps[n]
            if n >= ON_TENSOR:
                z_part = z_head if lo == 0 else z_tail
                nc.vector.scalar_tensor_tensor(
                    z_part[:, t, :], made[n, "least"][:], gain[:, t : t + 1], weighted_dist[t][:, lo:hi], ALU.mult, ALU.add
                )
                return
            blocks = hi // P
            over = bank_tile((7, 1)[n % 2], [P, blocks, P])
            for b in range(blocks):
                nc.tensor.transpose(over[:, b, :], made[n, "least"][:, b * P : (b + 1) * P], ident[:])
            turned_least = ring.tile([P, blocks, P], F32, name="turned_least")
            nc.scalar.copy(turned_least[:], over[:])
            total = bank_tile((0, 6)[n % 2], [P, hi])
            for b in range(blocks):
                add_transposes(total[:, b * P : (b + 1) * P], turned_dist[t][:, b, :], turned_least[:, b, :])
            nc.scalar.activation(z_head[:, t, :], total[:, :HEAD], ACT.Copy, scale=gain[:, t : t + 1])
            if hi > HEAD:
                nc.scalar.activation(z_tail[:, t, :], total[:, HEAD:], ACT.Copy, scale=gain[:, t : t + 1])

        def quantise_z(z_part, a, b, first_column, weave, tag):
            woven = keep.tile([P, b - a, PACK], BF16, name="woven%d" % first_column, tag=tag, align_bytes=64)
            weave(
                woven[:].rearrange("p (c i) t -> p c t i", i=PACK),
                z_part[:, :, a:b].rearrange("p t (c i) -> p c t i", i=PACK),
            )
            codes = keep.tile([P, b - a], U32, name="zcodes%d" % first_column, align_bytes=64)
            scales = keep.tile([P, b - a], U8, name="zscales%d" % first_column, align_bytes=64)
            nc.vector.quantize_mx(codes[:].bitcast(FP8X4), scales[:], woven[:].rearrange("p j t -> p (j t)"))
            return codes, scales

        def score(acc, block, zq):
            rows = slice(block * P, (block + 1) * P)
            nc.tensor.matmul_mx(
                out=acc,
                lhsT=picked_words["cand"][:, rows].bitcast(FP8X4),
                lhsT_scale=picked_scales["cand"][:, rows],
                rhs=zq[0][:].bitcast(FP8X4),
                rhs_scale=zq[1][:],
                start=True,
                stop=True,
            )

        def finish_head():
            number = 4
            for a, b in HEAD_PIECES:
                zq = quantise_z(z_head, a, b, a, nc.scalar.copy, "woven%d" % a)
                blocks = S // (b - a)
                rows = out[:, a:b].rearrange("(h b p) j -> h p b j", b=blocks, p=P)
                for h in range(C // P // blocks):
                    acc = bank_tile(number, [P, blocks, b - a])
                    for i in range(blocks):
                        score(acc[:, i, :], blocks * h + i, zq)
                    result = keep.tile([P, blocks, b - a], F32, name="result_head%d" % number)
                    nc.scalar.activation(result[:], acc[:], ACT.Copy, scale=OUT_SCALE)
                    nc.sync.dma_start(rows[h], result[:])
                    number = number + 1

        def finish_tail():
            zq = quantise_z(z_tail, 0, S - HEAD, HEAD, nc.vector.tensor_copy, "woven%d" % HEAD_PIECES[-1][0])
            rows = out[:, HEAD:].rearrange("(h b p) j -> h p b j", h=2, p=P)
            for h in range(2):
                result = keep.tile([P, 2, S - HEAD], F32, name="result_tail%d" % h)
                acc = bank_tile(2 + h, [P, 2, S - HEAD])
                for b in range(2):
                    score(acc[:, b, :], 2 * h + b, zq)
                if h == 0:
                    nc.scalar.activation(result[:], acc[:], ACT.Copy, scale=OUT_SCALE)
                    nc.scalar.dma_start(rows[h], result[:])
                else:
                    nc.vector.tensor_scalar_mul(result[:], acc[:], OUT_SCALE)
                    nc.sync.dma_start(rows[h], result[:])

        for n in range(last):
            cell(n, "di")
            if n > 0:
                least(n - 1)
            cell(n, "dj")
            if n > 0:
                weigh(n - 1)
            if n == first_tail:
                finish_head()
            cell(n, "dk")
            pair(n)
        cell(last, "di")
        cell(last, "dj")
        least(last - 1)
        pair(last)
        cell(last, "dk")
        weigh(last - 1)
        least(last)
        weigh(last)
        finish_tail()
